import numpy as np
import ml_dtypes


def mxq(x, axis, fmt="e4m3"):
    dtype, down = {"e4m3": (ml_dtypes.float8_e4m3fn, 7), "e5m2": (ml_dtypes.float8_e5m2, 14)}[fmt]
    v = np.moveaxis(np.asarray(x, np.float32).astype(ml_dtypes.bfloat16).astype(np.float64), axis, -1)
    blocks = v.reshape(v.shape[:-1] + (-1, 32))
    amax = np.abs(blocks).max(-1, keepdims=True)
    byte = np.maximum(np.where(amax > 0, np.frexp(amax)[1] - 1 + 127, 0) - down, 1)
    scale = np.exp2(byte - 127.0)
    codes = (blocks / scale).astype(np.float32).astype(dtype).astype(np.float64)
    return np.moveaxis((codes * scale).reshape(v.shape), -1, axis)


WIDE = False


def mx_kscale(k):
    if not WIDE:
        return np.ones(k)
    levels = np.array([10, -10, 5, -5, 0])
    if k % 512:
        return np.exp2(np.random.permutation(np.resize(levels, k // 32))).repeat(32)
    a = np.empty((k // 512, 16))
    for p in range(k // 512):
        a[p, :8] = np.random.permutation(np.resize(levels, 8))
        for g in range(8):
            far = levels[np.abs(levels - a[p, g]) >= 10]
            a[p, g + 8] = far[np.random.randint(len(far))]
    return np.exp2(a.ravel()).repeat(32)


def f64(x):
    return np.asarray(x).astype(np.float64)


def striped(idx):
    return np.tile(idx.reshape(-1, 16).T, (8, 1)).astype(np.uint16)


def unstriped(offs):
    return offs[:16].T.reshape(-1).astype(np.int64)


def pack_weight(w):
    k, n = w.shape
    w = f64(np.asarray(w, np.float32).astype(ml_dtypes.bfloat16)).reshape(k // 32, 32, n)
    amax = np.abs(w).max(1)
    byte = np.clip(np.where(amax > 0, np.frexp(amax)[1] - 1 + 127 - 7, 1), 1, 254)
    scaled = (w * np.exp2(127.0 - byte)[:, None, :]).reshape(k, n).astype(np.float32)
    words = np.ascontiguousarray(scaled.reshape(k // 512, 128, 4, n).transpose(0, 1, 3, 2)).astype(ml_dtypes.float8_e4m3fn).view(np.uint8)
    return words, np.ascontiguousarray(byte.astype(np.uint8).reshape(k // 512, 16, n))


def unpack_weight(words, scales):
    g, p, n, _ = words.shape
    vals = np.ascontiguousarray(words).view(ml_dtypes.float8_e4m3fn).astype(np.float64) * np.repeat(np.exp2(scales.astype(np.float64) - 127.0), 8, axis=1)[..., None]
    return vals.transpose(0, 1, 3, 2).reshape(g * 512, n)


def relu(v):
    return np.maximum(v, 0.0)


K, T, S, V, H = 512, 2048, 512, 512, 512


def setup_inputs():
    n = np.random.standard_normal
    s = mx_kscale(K)[:, None]
    packed_xT = pack_weight(n((K, T)) * s)
    return {
        "x_words": packed_xT[0],
        "x_scales": packed_xT[1],
        "w1": (n((K, H)) / np.sqrt(K) / s).astype(np.float32),
        "gs": (np.random.uniform(0.5, 1.5, (K, 1)) / s).astype(np.float32),
        "offs": striped(np.random.permutation(T)[:S]),
        "cand": striped(np.random.permutation(T)[:V]),
    }


def reference(x_words, x_scales, w1, gs, offs, cand):
    x_cand = unpack_weight(x_words, x_scales)[:, unstriped(cand)]
    xq = unpack_weight(x_words, x_scales)[:, unstriped(offs)]
    h = relu(mxq(f64(w1), 0, "e4m3").T @ xq)
    z = f64(gs) * h
    s = 0.0625 * ((x_cand.T @ mxq(z, 0, "e4m3")))
    return 4.0 * np.tanh(0.25 * s)

@@ -1,0 +1,170 @@
+from contextlib import ExitStack
+
+import concourse.mybir as mybir
+
+K, T, S, V, H = 512, 2048, 512, 512, 512
+FLOPS = 2 * K * H * S + 2 * K * V * S
+
+F32 = mybir.dt.float32
+BF16 = mybir.dt.bfloat16
+I32 = mybir.dt.int32
+U32 = mybir.dt.uint32
+U16 = mybir.dt.uint16
+U8 = mybir.dt.uint8
+FP8X4 = mybir.dt.float8_e4m3fn_x4
+ALU = mybir.AluOpType
+ACT = mybir.ActivationFunctionType
+
+P = 128
+PACK = 4
+CHUNK = 128
+HALF_M = 64
+W_COLS = 128
+
+
+def tile_picked_candcap_relu_p_kernel(tc, x_words, x_scales, w1, gs, offs, cand, out):
+    nc = tc.nc
+    with ExitStack() as ctx:
+        keep = ctx.enter_context(tc.tile_pool(name="keep", bufs=1))
+        psum = ctx.enter_context(tc.psum_pool(name="psum", bufs=1))
+
+        offs_sb = keep.tile([P, S // 16], U16, name="offs_sb")
+        cand_sb = keep.tile([P, V // 16], U16, name="cand_sb")
+        gs_sb = keep.tile([P, 1, PACK], F32, name="gs_sb")
+        table_bytes = keep.tile([P, T], U8, name="table_bytes", align_bytes=64)
+        table_words = keep.tile([P, T], I32, name="table_words", align_bytes=64)
+        warm = keep.tile([P, 1], F32, name="warm")
+        warm_out = keep.tile([P, 1], F32, name="warm_out")
+
+        nc.vector.memset(table_bytes[:, : 4 * 352].bitcast(I32), 0)
+        nc.gpsimd.memset(table_bytes[:, 4 * 352 :].bitcast(I32), 0)
+
+        w_rows = w1.rearrange("(p j) c -> p j c", j=PACK)
+        w_raw = [keep.tile([P, PACK, W_COLS], F32, name=f"w_raw{i}") for i in range(H // W_COLS)]
+
+        def load_w(i):
+            nc.sync.dma_start(w_raw[i][:], w_rows[:, :, i * W_COLS : (i + 1) * W_COLS])
+
+        nc.sync.dma_start(offs_sb[:], offs)
+        nc.sync.dma_start(cand_sb[:], cand)
+        load_w(0)
+        for q in range(4):
+            queue = nc.sync if q % 2 == 0 else nc.scalar
+            queue.dma_start(table_bytes[32 * q : 32 * q + 4, :].bitcast(I32), x_scales[0, 4 * q : 4 * q + 4, :].bitcast(I32))
+        nc.sync.dma_start(table_words[:], x_words[0].rearrange("p n t -> p (n t)").bitcast(I32))
+        for i in range(1, H // W_COLS):
+            load_w(i)
+        nc.sync.dma_start(gs_sb[:, 0, :], gs.rearrange("(p t) o -> p (t o)", t=PACK))
+        nc.vector.memset(warm[:], 0.0)
+        nc.scalar.activation(warm_out[:], warm[:], ACT.Tanh)
+
+        tok_bytes = keep.tile([P, S], U8, name="tok_bytes", align_bytes=64)
+        cand_bytes = keep.tile([P, V], U8, name="cand_bytes", align_bytes=64)
+        tok_words = keep.tile([P, S], U32, name="tok_words", align_bytes=64)
+        cand_words = {}
+        nc.vector.tensor_copy(tok_bytes[:], table_bytes[:].indirect(offs_sb[:]))
+        nc.vector.tensor_copy(cand_bytes[:], table_bytes[:].indirect(cand_sb[:]))
+        nc.vector.tensor_copy(tok_words[:], table_words[:].bitcast(U32).indirect(offs_sb[:]))
+
+        def gather_cand_words(half):
+            cand_words[half] = keep.tile([P, V // 2], U32, name=f"cand_words{half}", tag="w_bf1" if half else "cand_words0", align_bytes=64)
+            nc.vector.tensor_copy(
+                cand_words[half][:],
+                table_words[:].bitcast(U32).indirect(cand_sb[:, half * (V // 32) : (half + 1) * (V // 32)]),
+            )
+
+        w_words = keep.tile([P, H], U32, name="w_words", align_bytes=64)
+        w_bytes = keep.tile([P, H], U8, name="w_bytes", align_bytes=64)
+        w_bf = [keep.tile([P, PACK, HALF_M, PACK], BF16, name=f"w_bf{half}", tag=f"w_bf{half}", align_bytes=64) for half in range(2)]
+
+        def deal(i):
+            half, m0 = divmod(i * W_COLS // PACK, HALF_M)
+            nc.scalar.copy(
+                w_bf[half][:].rearrange("p t m j -> p m j t")[:, m0 : m0 + W_COLS // PACK],
+                w_raw[i][:].rearrange("p j (m t) -> p m j t", t=PACK),
+            )
+
+        def quantize_w(half):
+            for t in range(PACK):
+                cols = slice(P * t + HALF_M * half, P * t + HALF_M * (half + 1))
+                nc.vector.quantize_mx(
+                    out=w_words[:, cols].bitcast(FP8X4),
+                    scales=w_bytes[:, cols],
+                    in_=w_bf[half][:, t].rearrange("p m j -> p (m j)"),
+                )
+
+        for i in range(H // W_COLS):
+            deal(i)
+        gather_cand_words(0)
+        quantize_w(0)
+        quantize_w(1)
+        gather_cand_words(1)
+
+        chunks = S // CHUNK
+        z_bf, z_words, z_bytes, capped = {}, {}, {}, {}
+
+        def hidden(c):
+            cols = slice(c * CHUNK, (c + 1) * CHUNK)
+            bank = psum.tile([P, PACK, CHUNK], F32, name=f"h_bank{c}", tag=f"h_bank{c}")
+            for t in range(PACK):
+                nc.tensor.matmul_mx(
+                    out=bank[:, t, :],
+                    lhsT=w_words[:, P * t : P * (t + 1)].bitcast(FP8X4),
+                    lhsT_scale=w_bytes[:, P * t : P * (t + 1)],
+                    rhs=tok_words[:, cols].bitcast(FP8X4),
+                    rhs_scale=tok_bytes[:, cols],
+                    start=True,
+                    stop=True,
+                )
+            z_bf[c] = keep.tile([P, CHUNK, PACK], BF16, name=f"z_bf{c}", align_bytes=64)
+            nc.vector.scalar_tensor_tensor(
+                out=z_bf[c][:],
+                in0=bank[:].rearrange("p t n -> p n t"),
+                scalar=0.0,
+                in1=gs_sb[:].broadcast_to([P, CHUNK, PACK]),
+                op0=ALU.max,
+                op1=ALU.mult,
+            )
+
+        def quantize_z(c):
+            z_words[c] = keep.tile([P, CHUNK], U32, name=f"z_words{c}", align_bytes=64)
+            z_bytes[c] = keep.tile([P, CHUNK], U8, name=f"z_bytes{c}", align_bytes=64)
+            nc.vector.quantize_mx(
+                out=z_words[c][:].bitcast(FP8X4),
+                scales=z_bytes[c][:],
+                in_=z_bf[c][:].rearrange("p n t -> p (n t)"),
+            )
+
+        def score(c, v0, v1):
+            bank = psum.tile([P, v1 - v0, CHUNK], F32, name=f"s_bank{c}_{v0}", tag="h_bank0" if v0 else f"s_bank{c}")
+            for v in range(v0, v1):
+                nc.tensor.matmul_mx(
+                    out=bank[:, v - v0, :],
+                    lhsT=cand_words[v // 2][:, P * (v % 2) : P * (v % 2 + 1)].bitcast(FP8X4),
+                    lhsT_scale=cand_bytes[:, P * v : P * (v + 1)],
+                    rhs=z_words[c][:].bitcast(FP8X4),
+                    rhs_scale=z_bytes[c][:],
+                    start=True,
+                    stop=True,
+                )
+            capped[c, v0] = keep.tile([P, v1 - v0, CHUNK], F32, name=f"capped{c}_{v0}")
+            nc.scalar.activation(capped[c, v0][:], bank[:], ACT.Tanh, scale=0.25 * 0.0625)
+
+        def leave(c, v0, v1):
+            result = keep.tile([P, v1 - v0, CHUNK], F32, name=f"result{c}_{v0}")
+            nc.vector.tensor_scalar_mul(result[:], capped[c, v0][:], 4.0)
+            nc.sync.dma_start(out.rearrange("(v p) s -> p v s", p=P)[:, v0:v1, c * CHUNK : (c + 1) * CHUNK], result[:])
+
+        def pieces(c):
+            return [(0, 2), (2, 4)] if c == chunks - 1 else [(0, 4)]
+
+        hidden(0)
+        for c in range(chunks):
+            if c + 1 < chunks:
+                hidden(c + 1)
+            quantize_z(c)
+            for v0, v1 in pieces(c):
+                score(c, v0, v1)
+        for c in range(chunks):
+            for v0, v1 in pieces(c):
+                leave(c, v0, v1)

@@ -19,7 +19,9 @@ P = 128
 PACK = 4
 CHUNK = 128
 HALF_M = 64
-W_COLS = 128
+W_COLS = 256
+SCALAR_M = 32
+EARLY_T = 512
 
 
 def tile_picked_candcap_relu_p_kernel(tc, x_words, x_scales, w1, gs, offs, cand, out):
@@ -47,12 +49,13 @@ def tile_picked_candcap_relu_p_kernel(tc, x_words, x_scales, w1, gs, offs, cand,
 
         nc.sync.dma_start(offs_sb[:], offs)
         nc.sync.dma_start(cand_sb[:], cand)
-        load_w(0)
+        table_rows = x_words[0].rearrange("p n t -> p (n t)").bitcast(I32)
+        nc.sync.dma_start(table_words[:, :EARLY_T], table_rows[:, :EARLY_T])
         for q in range(4):
             queue = nc.sync if q % 2 == 0 else nc.scalar
             queue.dma_start(table_bytes[32 * q : 32 * q + 4, :].bitcast(I32), x_scales[0, 4 * q : 4 * q + 4, :].bitcast(I32))
-        nc.sync.dma_start(table_words[:], x_words[0].rearrange("p n t -> p (n t)").bitcast(I32))
-        for i in range(1, H // W_COLS):
+        nc.sync.dma_start(table_words[:, EARLY_T:], table_rows[:, EARLY_T:])
+        for i in range(H // W_COLS):
             load_w(i)
         nc.sync.dma_start(gs_sb[:, 0, :], gs.rearrange("(p t) o -> p (t o)", t=PACK))
         nc.vector.memset(warm[:], 0.0)
@@ -77,11 +80,10 @@ def tile_picked_candcap_relu_p_kernel(tc, x_words, x_scales, w1, gs, offs, cand,
         w_bytes = keep.tile([P, H], U8, name="w_bytes", align_bytes=64)
         w_bf = [keep.tile([P, PACK, HALF_M, PACK], BF16, name=f"w_bf{half}", tag=f"w_bf{half}", align_bytes=64) for half in range(2)]
 
-        def deal(i):
-            half, m0 = divmod(i * W_COLS // PACK, HALF_M)
-            nc.scalar.copy(
-                w_bf[half][:].rearrange("p t m j -> p m j t")[:, m0 : m0 + W_COLS // PACK],
-                w_raw[i][:].rearrange("p j (m t) -> p m j t", t=PACK),
+        def deal(copy, half, m0, m1):
+            copy(
+                w_bf[half][:].rearrange("p t m j -> p m t j")[:, m0:m1],
+                w_raw[half][:].rearrange("p j (m t) -> p m t j", t=PACK)[:, m0:m1],
             )
 
         def quantize_w(half):
@@ -93,9 +95,10 @@ def tile_picked_candcap_relu_p_kernel(tc, x_words, x_scales, w1, gs, offs, cand,
                     in_=w_bf[half][:, t].rearrange("p m j -> p (m j)"),
                 )
 
-        for i in range(H // W_COLS):
-            deal(i)
+        deal(nc.scalar.copy, 0, 0, HALF_M)
+        deal(nc.scalar.copy, 1, 0, SCALAR_M)
         gather_cand_words(0)
+        deal(nc.vector.tensor_copy, 1, SCALAR_M, HALF_M)
         quantize_w(0)
         quantize_w(1)
         gather_cand_words(1)

@@ -17,11 +17,13 @@ ACT = mybir.ActivationFunctionType
 
 P = 128
 PACK = 4
+BLOCK_P = 8
+QUADRANT = 32
+LIST_P = 16
 CHUNK = 128
-HALF_M = 64
-W_COLS = 256
-SCALAR_M = 32
-EARLY_T = 512
+CHUNKS = S // CHUNK
+V_TILES = V // P
+SCALAR_M = 64
 
 
 def tile_picked_candcap_relu_p_kernel(tc, x_words, x_scales, w1, gs, offs, cand, out):
@@ -30,81 +32,58 @@ def tile_picked_candcap_relu_p_kernel(tc, x_words, x_scales, w1, gs, offs, cand,
         keep = ctx.enter_context(tc.tile_pool(name="keep", bufs=1))
         psum = ctx.enter_context(tc.psum_pool(name="psum", bufs=1))
 
-        offs_sb = keep.tile([P, S // 16], U16, name="offs_sb")
-        cand_sb = keep.tile([P, V // 16], U16, name="cand_sb")
+        offs_sb = keep.tile([P, S // LIST_P], U16, name="offs_sb")
+        cand_sb = keep.tile([P, V // LIST_P], U16, name="cand_sb")
         gs_sb = keep.tile([P, 1, PACK], F32, name="gs_sb")
         table_bytes = keep.tile([P, T], U8, name="table_bytes", align_bytes=64)
         table_words = keep.tile([P, T], I32, name="table_words", align_bytes=64)
-        warm = keep.tile([P, 1], F32, name="warm")
-        warm_out = keep.tile([P, 1], F32, name="warm_out")
+        w_raw = keep.tile([P, PACK, H], F32, name="w_raw")
+        scale_planes = keep.tile([P, S + V], U8, name="scale_planes", align_bytes=64)
 
-        nc.vector.memset(table_bytes[:, : 4 * 352].bitcast(I32), 0)
-        nc.gpsimd.memset(table_bytes[:, 4 * 352 :].bitcast(I32), 0)
-
-        w_rows = w1.rearrange("(p j) c -> p j c", j=PACK)
-        w_raw = [keep.tile([P, PACK, W_COLS], F32, name=f"w_raw{i}") for i in range(H // W_COLS)]
-
-        def load_w(i):
-            nc.sync.dma_start(w_raw[i][:], w_rows[:, :, i * W_COLS : (i + 1) * W_COLS])
-
+        nc.vector.memset(table_bytes[:].bitcast(I32), 0)
         nc.sync.dma_start(offs_sb[:], offs)
         nc.sync.dma_start(cand_sb[:], cand)
-        table_rows = x_words[0].rearrange("p n t -> p (n t)").bitcast(I32)
-        nc.sync.dma_start(table_words[:, :EARLY_T], table_rows[:, :EARLY_T])
-        for q in range(4):
-            queue = nc.sync if q % 2 == 0 else nc.scalar
-            queue.dma_start(table_bytes[32 * q : 32 * q + 4, :].bitcast(I32), x_scales[0, 4 * q : 4 * q + 4, :].bitcast(I32))
-        nc.sync.dma_start(table_words[:, EARLY_T:], table_rows[:, EARLY_T:])
-        for i in range(H // W_COLS):
-            load_w(i)
         nc.sync.dma_start(gs_sb[:, 0, :], gs.rearrange("(p t) o -> p (t o)", t=PACK))
-        nc.vector.memset(warm[:], 0.0)
-        nc.scalar.activation(warm_out[:], warm[:], ACT.Tanh)
+        nc.sync.dma_start(table_bytes[0:P:BLOCK_P, :].bitcast(I32), x_scales[0].bitcast(I32))
+        nc.sync.dma_start(w_raw[:], w1.rearrange("(p j) c -> p j c", j=PACK))
+        nc.sync.dma_start(table_words[:], x_words[0].rearrange("p n t -> p (n t)").bitcast(I32))
 
-        tok_bytes = keep.tile([P, S], U8, name="tok_bytes", align_bytes=64)
-        cand_bytes = keep.tile([P, V], U8, name="cand_bytes", align_bytes=64)
-        tok_words = keep.tile([P, S], U32, name="tok_words", align_bytes=64)
-        cand_words = {}
-        nc.vector.tensor_copy(tok_bytes[:], table_bytes[:].indirect(offs_sb[:]))
-        nc.vector.tensor_copy(cand_bytes[:], table_bytes[:].indirect(cand_sb[:]))
-        nc.vector.tensor_copy(tok_words[:], table_words[:].bitcast(U32).indirect(offs_sb[:]))
+        preload_in = keep.tile([P, 1], F32, name="preload_in")
+        preload_out = keep.tile([P, 1], F32, name="preload_out")
+        nc.vector.memset(preload_in[:], 0.0)
+        nc.scalar.activation(preload_out[:], preload_in[:], ACT.Tanh)
 
-        def gather_cand_words(half):
-            cand_words[half] = keep.tile([P, V // 2], U32, name=f"cand_words{half}", tag="w_bf1" if half else "cand_words0", align_bytes=64)
-            nc.vector.tensor_copy(
-                cand_words[half][:],
-                table_words[:].bitcast(U32).indirect(cand_sb[:, half * (V // 32) : (half + 1) * (V // 32)]),
+        nc.vector.memset(scale_planes[:].bitcast(I32), 0)
+        picked_bytes = keep.tile([P, S + V], U8, name="picked_bytes", align_bytes=64)
+        nc.vector.tensor_copy(picked_bytes[:, :S], table_bytes[:].indirect(offs_sb[:]))
+        nc.vector.tensor_copy(picked_bytes[:, S:], table_bytes[:].indirect(cand_sb[:]))
+        for i in range(QUADRANT // BLOCK_P):
+            nc.sync.dma_start(
+                scale_planes[i:P:QUADRANT, :].bitcast(I32),
+                picked_bytes[BLOCK_P * i : P : QUADRANT, :].bitcast(I32),
             )
+        tok_plane = scale_planes[:, :S]
+        cand_plane = scale_planes[:, S:]
 
+        w_bf = keep.tile([P, PACK, P, PACK], BF16, name="w_bf", align_bytes=64)
         w_words = keep.tile([P, H], U32, name="w_words", align_bytes=64)
-        w_bytes = keep.tile([P, H], U8, name="w_bytes", align_bytes=64)
-        w_bf = [keep.tile([P, PACK, HALF_M, PACK], BF16, name=f"w_bf{half}", tag=f"w_bf{half}", align_bytes=64) for half in range(2)]
+        w_plane = keep.tile([P, H], U8, name="w_plane", align_bytes=64)
+        dealt = w_bf[:].rearrange("p t m j -> p m t j")
+        loaded = w_raw[:].rearrange("p j (m t) -> p m t j", t=PACK)
+        nc.scalar.copy(dealt[:, :SCALAR_M], loaded[:, :SCALAR_M])
+        nc.vector.tensor_copy(dealt[:, SCALAR_M:], loaded[:, SCALAR_M:])
+        nc.vector.quantize_mx(
+            out=w_words[:].bitcast(FP8X4),
+            scales=w_plane[:],
+            in_=w_bf[:].rearrange("p t m j -> p (t m j)"),
+        )
 
-        def deal(copy, half, m0, m1):
-            copy(
-                w_bf[half][:].rearrange("p t m j -> p m t j")[:, m0:m1],
-                w_raw[half][:].rearrange("p j (m t) -> p m t j", t=PACK)[:, m0:m1],
-            )
+        tok_words = keep.tile([P, S], U32, name="tok_words", align_bytes=64)
+        cand_words = keep.tile([P, V], U32, name="cand_words", align_bytes=64)
+        nc.vector.tensor_copy(tok_words[:], table_words[:].bitcast(U32).indirect(offs_sb[:]))
+        nc.vector.tensor_copy(cand_words[:], table_words[:].bitcast(U32).indirect(cand_sb[:]))
 
-        def quantize_w(half):
-            for t in range(PACK):
-                cols = slice(P * t + HALF_M * half, P * t + HALF_M * (half + 1))
-                nc.vector.quantize_mx(
-                    out=w_words[:, cols].bitcast(FP8X4),
-                    scales=w_bytes[:, cols],
-                    in_=w_bf[half][:, t].rearrange("p m j -> p (m j)"),
-                )
-
-        deal(nc.scalar.copy, 0, 0, HALF_M)
-        deal(nc.scalar.copy, 1, 0, SCALAR_M)
-        gather_cand_words(0)
-        deal(nc.vector.tensor_copy, 1, SCALAR_M, HALF_M)
-        quantize_w(0)
-        quantize_w(1)
-        gather_cand_words(1)
-
-        chunks = S // CHUNK
-        z_bf, z_words, z_bytes, capped = {}, {}, {}, {}
+        z_bf, z_words, z_plane, capped = {}, {}, {}, {}
 
         def hidden(c):
             cols = slice(c * CHUNK, (c + 1) * CHUNK)
@@ -113,9 +92,9 @@ def tile_picked_candcap_relu_p_kernel(tc, x_words, x_scales, w1, gs, offs, cand,
                 nc.tensor.matmul_mx(
                     out=bank[:, t, :],
                     lhsT=w_words[:, P * t : P * (t + 1)].bitcast(FP8X4),
-                    lhsT_scale=w_bytes[:, P * t : P * (t + 1)],
+                    lhsT_scale=w_plane[:, P * t : P * (t + 1)],
                     rhs=tok_words[:, cols].bitcast(FP8X4),
-                    rhs_scale=tok_bytes[:, cols],
+                    rhs_scale=tok_plane[:, cols],
                     start=True,
                     stop=True,
                 )
@@ -131,10 +110,10 @@ def tile_picked_candcap_relu_p_kernel(tc, x_words, x_scales, w1, gs, offs, cand,
 
         def quantize_z(c):
             z_words[c] = keep.tile([P, CHUNK], U32, name=f"z_words{c}", align_bytes=64)
-            z_bytes[c] = keep.tile([P, CHUNK], U8, name=f"z_bytes{c}", align_bytes=64)
+            z_plane[c] = keep.tile([P, CHUNK], U8, name=f"z_plane{c}", align_bytes=64)
             nc.vector.quantize_mx(
                 out=z_words[c][:].bitcast(FP8X4),
-                scales=z_bytes[c][:],
+                scales=z_plane[c][:],
                 in_=z_bf[c][:].rearrange("p n t -> p (n t)"),
             )
 
@@ -143,10 +122,10 @@ def tile_picked_candcap_relu_p_kernel(tc, x_words, x_scales, w1, gs, offs, cand,
             for v in range(v0, v1):
                 nc.tensor.matmul_mx(
                     out=bank[:, v - v0, :],
-                    lhsT=cand_words[v // 2][:, P * (v % 2) : P * (v % 2 + 1)].bitcast(FP8X4),
-                    lhsT_scale=cand_bytes[:, P * v : P * (v + 1)],
+                    lhsT=cand_words[:, P * v : P * (v + 1)].bitcast(FP8X4),
+                    lhsT_scale=cand_plane[:, P * v : P * (v + 1)],
                     rhs=z_words[c][:].bitcast(FP8X4),
-                    rhs_scale=z_bytes[c][:],
+                    rhs_scale=z_plane[c][:],
                     start=True,
                     stop=True,
                 )
@@ -159,15 +138,16 @@ def tile_picked_candcap_relu_p_kernel(tc, x_words, x_scales, w1, gs, offs, cand,
             nc.sync.dma_start(out.rearrange("(v p) s -> p v s", p=P)[:, v0:v1, c * CHUNK : (c + 1) * CHUNK], result[:])
 
         def pieces(c):
-            return [(0, 2), (2, 4)] if c == chunks - 1 else [(0, 4)]
+            half = V_TILES // 2
+            return [(0, half), (half, V_TILES)] if c == CHUNKS - 1 else [(0, V_TILES)]
 
         hidden(0)
-        for c in range(chunks):
-            if c + 1 < chunks:
+        for c in range(CHUNKS):
+            if c + 1 < CHUNKS:
                 hidden(c + 1)
             quantize_z(c)
             for v0, v1 in pieces(c):
                 score(c, v0, v1)
-        for c in range(chunks):
+        for c in range(CHUNKS):
             for v0, v1 in pieces(c):
                 leave(c, v0, v1)

from contextlib import ExitStack

import concourse.mybir as mybir

K, T, S, V, H = 512, 2048, 512, 512, 512
FLOPS = 2 * K * H * S + 2 * K * V * S

F32 = mybir.dt.float32
BF16 = mybir.dt.bfloat16
I32 = mybir.dt.int32
U32 = mybir.dt.uint32
U16 = mybir.dt.uint16
U8 = mybir.dt.uint8
FP8X4 = mybir.dt.float8_e4m3fn_x4
ALU = mybir.AluOpType
ACT = mybir.ActivationFunctionType

P = 128
PACK = 4
BLOCK_P = 8
QUADRANT = 32
LIST_P = 16
CHUNK = 128
CHUNKS = S // CHUNK
V_TILES = V // P
SCALAR_M = 64


def tile_picked_candcap_relu_p_kernel(tc, x_words, x_scales, w1, gs, offs, cand, out):
    nc = tc.nc
    with ExitStack() as ctx:
        keep = ctx.enter_context(tc.tile_pool(name="keep", bufs=1))
        psum = ctx.enter_context(tc.psum_pool(name="psum", bufs=1))

        offs_sb = keep.tile([P, S // LIST_P], U16, name="offs_sb")
        cand_sb = keep.tile([P, V // LIST_P], U16, name="cand_sb")
        gs_sb = keep.tile([P, 1, PACK], F32, name="gs_sb")
        table_bytes = keep.tile([P, T], U8, name="table_bytes", align_bytes=64)
        table_words = keep.tile([P, T], I32, name="table_words", align_bytes=64)
        w_raw = keep.tile([P, PACK, H], F32, name="w_raw")
        scale_planes = keep.tile([P, S + V], U8, name="scale_planes", align_bytes=64)

        nc.vector.memset(table_bytes[:].bitcast(I32), 0)
        nc.sync.dma_start(offs_sb[:], offs)
        nc.sync.dma_start(cand_sb[:], cand)
        nc.sync.dma_start(gs_sb[:, 0, :], gs.rearrange("(p t) o -> p (t o)", t=PACK))
        nc.sync.dma_start(table_bytes[0:P:BLOCK_P, :].bitcast(I32), x_scales[0].bitcast(I32))
        nc.sync.dma_start(w_raw[:], w1.rearrange("(p j) c -> p j c", j=PACK))
        nc.sync.dma_start(table_words[:], x_words[0].rearrange("p n t -> p (n t)").bitcast(I32))

        preload_in = keep.tile([P, 1], F32, name="preload_in")
        preload_out = keep.tile([P, 1], F32, name="preload_out")
        nc.vector.memset(preload_in[:], 0.0)
        nc.scalar.activation(preload_out[:], preload_in[:], ACT.Tanh)

        nc.vector.memset(scale_planes[:].bitcast(I32), 0)
        picked_bytes = keep.tile([P, S + V], U8, name="picked_bytes", align_bytes=64)
        nc.vector.tensor_copy(picked_bytes[:, :S], table_bytes[:].indirect(offs_sb[:]))
        nc.vector.tensor_copy(picked_bytes[:, S:], table_bytes[:].indirect(cand_sb[:]))
        for i in range(QUADRANT // BLOCK_P):
            nc.sync.dma_start(
                scale_planes[i:P:QUADRANT, :].bitcast(I32),
                picked_bytes[BLOCK_P * i : P : QUADRANT, :].bitcast(I32),
            )
        tok_plane = scale_planes[:, :S]
        cand_plane = scale_planes[:, S:]

        w_bf = keep.tile([P, PACK, P, PACK], BF16, name="w_bf", align_bytes=64)
        w_words = keep.tile([P, H], U32, name="w_words", align_bytes=64)
        w_plane = keep.tile([P, H], U8, name="w_plane", align_bytes=64)
        dealt = w_bf[:].rearrange("p t m j -> p m t j")
        loaded = w_raw[:].rearrange("p j (m t) -> p m t j", t=PACK)
        nc.scalar.copy(dealt[:, :SCALAR_M], loaded[:, :SCALAR_M])
        nc.vector.tensor_copy(dealt[:, SCALAR_M:], loaded[:, SCALAR_M:])
        nc.vector.quantize_mx(
            out=w_words[:].bitcast(FP8X4),
            scales=w_plane[:],
            in_=w_bf[:].rearrange("p t m j -> p (t m j)"),
        )

        tok_words = keep.tile([P, S], U32, name="tok_words", align_bytes=64)
        cand_words = keep.tile([P, V], U32, name="cand_words", align_bytes=64)
        nc.vector.tensor_copy(tok_words[:], table_words[:].bitcast(U32).indirect(offs_sb[:]))
        nc.vector.tensor_copy(cand_words[:], table_words[:].bitcast(U32).indirect(cand_sb[:]))

        z_bf, z_words, z_plane, capped = {}, {}, {}, {}

        def hidden(c):
            cols = slice(c * CHUNK, (c + 1) * CHUNK)
            bank = psum.tile([P, PACK, CHUNK], F32, name=f"h_bank{c}", tag=f"h_bank{c}")
            for t in range(PACK):
                nc.tensor.matmul_mx(
                    out=bank[:, t, :],
                    lhsT=w_words[:, P * t : P * (t + 1)].bitcast(FP8X4),
                    lhsT_scale=w_plane[:, P * t : P * (t + 1)],
                    rhs=tok_words[:, cols].bitcast(FP8X4),
                    rhs_scale=tok_plane[:, cols],
                    start=True,
                    stop=True,
                )
            z_bf[c] = keep.tile([P, CHUNK, PACK], BF16, name=f"z_bf{c}", align_bytes=64)
            nc.vector.scalar_tensor_tensor(
                out=z_bf[c][:],
                in0=bank[:].rearrange("p t n -> p n t"),
                scalar=0.0,
                in1=gs_sb[:].broadcast_to([P, CHUNK, PACK]),
                op0=ALU.max,
                op1=ALU.mult,
            )

        def quantize_z(c):
            z_words[c] = keep.tile([P, CHUNK], U32, name=f"z_words{c}", align_bytes=64)
            z_plane[c] = keep.tile([P, CHUNK], U8, name=f"z_plane{c}", align_bytes=64)
            nc.vector.quantize_mx(
                out=z_words[c][:].bitcast(FP8X4),
                scales=z_plane[c][:],
                in_=z_bf[c][:].rearrange("p n t -> p (n t)"),
            )

        def score(c, v0, v1):
            bank = psum.tile([P, v1 - v0, CHUNK], F32, name=f"s_bank{c}_{v0}", tag="h_bank0" if v0 else f"s_bank{c}")
            for v in range(v0, v1):
                nc.tensor.matmul_mx(
                    out=bank[:, v - v0, :],
                    lhsT=cand_words[:, P * v : P * (v + 1)].bitcast(FP8X4),
                    lhsT_scale=cand_plane[:, P * v : P * (v + 1)],
                    rhs=z_words[c][:].bitcast(FP8X4),
                    rhs_scale=z_plane[c][:],
                    start=True,
                    stop=True,
                )
            capped[c, v0] = keep.tile([P, v1 - v0, CHUNK], F32, name=f"capped{c}_{v0}")
            nc.scalar.activation(capped[c, v0][:], bank[:], ACT.Tanh, scale=0.25 * 0.0625)

        def leave(c, v0, v1):
            result = keep.tile([P, v1 - v0, CHUNK], F32, name=f"result{c}_{v0}")
            nc.vector.tensor_scalar_mul(result[:], capped[c, v0][:], 4.0)
            nc.sync.dma_start(out.rearrange("(v p) s -> p v s", p=P)[:, v0:v1, c * CHUNK : (c + 1) * CHUNK], result[:])

        def pieces(c):
            half = V_TILES // 2
            return [(0, half), (half, V_TILES)] if c == CHUNKS - 1 else [(0, V_TILES)]

        hidden(0)
        for c in range(CHUNKS):
            if c + 1 < CHUNKS:
                hidden(c + 1)
            quantize_z(c)
            for v0, v1 in pieces(c):
                score(c, v0, v1)
        for c in range(CHUNKS):
            for v0, v1 in pieces(c):
                leave(c, v0, v1)
